import numpy as np
import ml_dtypes


def mxq(x, axis, fmt="e4m3"):
    dtype, down = {"e4m3": (ml_dtypes.float8_e4m3fn, 7), "e5m2": (ml_dtypes.float8_e5m2, 14)}[fmt]
    v = np.moveaxis(np.asarray(x, np.float32).astype(ml_dtypes.bfloat16).astype(np.float64), axis, -1)
    blocks = v.reshape(v.shape[:-1] + (-1, 32))
    amax = np.abs(blocks).max(-1, keepdims=True)
    byte = np.maximum(np.where(amax > 0, np.frexp(amax)[1] - 1 + 127, 0) - down, 1)
    scale = np.exp2(byte - 127.0)
    codes = (blocks / scale).astype(np.float32).astype(dtype).astype(np.float64)
    return np.moveaxis((codes * scale).reshape(v.shape), -1, axis)


WIDE = False


def mx_kscale(k):
    if not WIDE:
        return np.ones(k)
    levels = np.array([10, -10, 5, -5, 0])
    if k % 512:
        return np.exp2(np.random.permutation(np.resize(levels, k // 32))).repeat(32)
    a = np.empty((k // 512, 16))
    for p in range(k // 512):
        a[p, :8] = np.random.permutation(np.resize(levels, 8))
        for g in range(8):
            far = levels[np.abs(levels - a[p, g]) >= 10]
            a[p, g + 8] = far[np.random.randint(len(far))]
    return np.exp2(a.ravel()).repeat(32)


def f64(x):
    return np.asarray(x).astype(np.float64)


def striped(idx):
    return np.tile(idx.reshape(-1, 16).T, (8, 1)).astype(np.uint16)


def unstriped(offs):
    return offs[:16].T.reshape(-1).astype(np.int64)


def striped8(idx):
    return np.concatenate([x.reshape(-1, 16).T for x in idx]).astype(np.uint16)


def runs(offs, k):
    lists = np.stack([offs[16 * r : 16 * r + 16].T.reshape(-1) for r in range(8)]).astype(np.int64)
    return lists[np.arange(k) % 512 // 64]


def pack_weight(w):
    k, n = w.shape
    w = f64(np.asarray(w, np.float32).astype(ml_dtypes.bfloat16)).reshape(k // 32, 32, n)
    amax = np.abs(w).max(1)
    byte = np.clip(np.where(amax > 0, np.frexp(amax)[1] - 1 + 127 - 7, 1), 1, 254)
    scaled = (w * np.exp2(127.0 - byte)[:, None, :]).reshape(k, n).astype(np.float32)
    words = np.ascontiguousarray(scaled.reshape(k // 512, 128, 4, n).transpose(0, 1, 3, 2)).astype(ml_dtypes.float8_e4m3fn).view(np.uint8)
    return words, np.ascontiguousarray(byte.astype(np.uint8).reshape(k // 512, 16, n))


def unpack_weight(words, scales):
    g, p, n, _ = words.shape
    vals = np.ascontiguousarray(words).view(ml_dtypes.float8_e4m3fn).astype(np.float64) * np.repeat(np.exp2(scales.astype(np.float64) - 127.0), 8, axis=1)[..., None]
    return vals.transpose(0, 1, 3, 2).reshape(g * 512, n)


K, T, S, H, W, G, U = 512, 1024, 256, 512, 128, 2048, 512


def setup_inputs():
    n = np.random.standard_normal
    s = mx_kscale(K)[:, None]
    packed_xT = pack_weight(n((K, T)) * s)
    packed_dT = pack_weight(n((K, G)) / s)
    perm = np.random.permutation(S)
    perm2 = np.random.permutation(S)
    perm3 = np.random.permutation(U)
    return {
        "x_words": packed_xT[0],
        "x_scales": packed_xT[1],
        "w1": (n((K, H)) / np.sqrt(2 * K) / s).astype(np.float32),
        "w2": (n((K, H)) / np.sqrt(2 * K) / s).astype(np.float32),
        "gs": (np.random.uniform(0.5, 1.5, (K, 1)) * s).astype(np.float32),
        "d_words": packed_dT[0],
        "d_scales": packed_dT[1],
        "offs": striped(np.random.permutation(T)[:S]),
        "two": striped(np.random.permutation(T)[:S]),
        "n1": striped(perm[:W]),
        "n2": striped(perm[W:]),
        "n3": striped(perm2[:W]),
        "n4": striped(perm2[W:]),
        "n5": striped(np.random.permutation(S)),
        "ka": striped8(np.random.randint(0, G, (8, H))),
        "kb": striped8(np.random.randint(0, G, (8, H))),
        "n6": striped(perm3[:S]),
        "n7": striped(perm3[S:]),
        "n8": striped(np.random.permutation(S)),
    }


def reference(x_words, x_scales, w1, w2, gs, d_words, d_scales, offs, two, n1, n2, n3, n4, n5, ka, kb, n6, n7, n8):
    d_ka = unpack_weight(d_words, d_scales)[np.arange(K)[:, None], runs(ka, K)]
    xq = unpack_weight(x_words, x_scales)[:, unstriped(offs)]
    x_two = unpack_weight(x_words, x_scales)[:, unstriped(two)]
    y = mxq(f64(w1), 0, "e4m3").T @ xq + mxq(f64(w2), 0, "e4m3").T @ x_two
    pa = y[:, unstriped(n1)]
    pb = y[:, unstriped(n2)]
    rb = np.maximum(pa, pb)
    ra = pa + pb
    ua = np.zeros((H, S))
    ua[:, unstriped(n3)] = ra
    ub = ua.copy()
    ub[:, unstriped(n4)] = rb
    z = f64(gs) * (ub - ub[:, unstriped(n5)])
    zq = mxq(z, 0, "e4m3")
    d_kb = unpack_weight(d_words, d_scales)[np.arange(K)[:, None], runs(kb, K)]
    h2 = 0.0625 * (d_ka.T @ zq + d_kb.T @ zq)
    dn = np.minimum(h2, h2[:, unstriped(n8)])
    up = np.maximum(h2, h2[:, unstriped(n8)])
    ph = np.zeros((H, U))
    ph[:, unstriped(n6)] = up
    out = ph.copy()
    out[:, unstriped(n7)] = dn
    return out

@@ -1,0 +1,312 @@
+from contextlib import ExitStack
+
+import concourse.mybir as mybir
+
+K, T, S, H, W, G, U = 512, 1024, 256, 512, 128, 2048, 512
+FLOPS = 2 * (2 * K * H * S) + 2 * (2 * K * H * S)
+
+F32 = mybir.dt.float32
+BF16 = mybir.dt.bfloat16
+I32 = mybir.dt.int32
+U32 = mybir.dt.uint32
+U16 = mybir.dt.uint16
+U8 = mybir.dt.uint8
+FP8X4 = mybir.dt.float8_e4m3fn_x4
+ALU = mybir.AluOpType
+COPY = mybir.ActivationFunctionType.Copy
+
+P = 128
+PACK = 4
+HALF = 64
+
+
+def tile_picked_dttzacphdpagmx_none_p_kernel(
+    tc, x_words, x_scales, w1, w2, gs, d_words, d_scales, offs, two, n1, n2, n3, n4, n5, ka, kb, n6, n7, n8, out
+):
+    nc = tc.nc
+    with ExitStack() as ctx:
+        keep = ctx.enter_context(tc.tile_pool(name="keep", bufs=1))
+        psum = ctx.enter_context(tc.psum_pool(name="psum", bufs=1))
+
+        def sb(name, shape, dtype, tag=""):
+            return keep.tile(shape, dtype, name=name, tag=tag or name, align_bytes=64)
+
+        def load_list(name, src):
+            tile = keep.tile(list(src.shape), U16, name=name)
+            nc.sync.dma_start(tile[:], src)
+            return tile
+
+        def load_weight_half(name, w, half, queue):
+            raw = sb(name, [P, PACK, H // 2], F32)
+            cols = slice(half * (H // 2), (half + 1) * (H // 2))
+            queue.dma_start(raw[:], w.rearrange("(p j) c -> p j c", j=PACK)[:, :, cols])
+            return raw
+
+        xs_table = sb("xs_table", [P, T], U8)
+        nc.gpsimd.memset(xs_table[:].bitcast(I32), 0)
+        offs_t = load_list("offs_t", offs)
+        two_t = load_list("two_t", two)
+        xw_table = sb("xw_table", [P, T], I32)
+        nc.sync.dma_start(xw_table[:], x_words[0].rearrange("p n t -> p (n t)").bitcast(I32))
+        xs_rows = x_scales[0].bitcast(I32)
+        for r in range(4):
+            nc.scalar.dma_start(xs_table[r:P:32, :].bitcast(I32), xs_rows[r:16:4, :])
+        raw = {}
+        raw[0, 0] = load_weight_half("w1_lo", w1, 0, nc.sync)
+        raw[1, 0] = load_weight_half("w2_lo", w2, 0, nc.sync)
+        n1_t = load_list("n1_t", n1)
+        n2_t = load_list("n2_t", n2)
+        raw[0, 1] = load_weight_half("w1_hi", w1, 1, nc.sync)
+        raw[1, 1] = load_weight_half("w2_hi", w2, 1, nc.sync)
+        n3_t = load_list("n3_t", n3)
+        n4_t = load_list("n4_t", n4)
+        ka_t = load_list("ka_t", ka)
+        kb_t = load_list("kb_t", kb)
+        ds_table = sb("ds_table", [P, G], U8)
+        nc.vector.memset(ds_table[:].bitcast(I32), 0)
+        ds_rows = d_scales[0].bitcast(I32)
+        for e in range(2):
+            nc.sync.dma_start(ds_table[e:P:16, :].bitcast(I32), ds_rows[e:16:2, :])
+        dw_table = sb("dw_table", [P, G], I32)
+        nc.sync.dma_start(dw_table[:], d_words[0].rearrange("p n t -> p (n t)").bitcast(I32))
+        gs_t = sb("gs_t", [P, PACK], F32)
+        nc.sync.dma_start(gs_t[:], gs.rearrange("(p t) o -> p (t o)", t=PACK))
+        n5_t = load_list("n5_t", n5)
+        n8_t = load_list("n8_t", n8)
+        n6_t = load_list("n6_t", n6)
+        n7_t = load_list("n7_t", n7)
+
+        x_codes, x_bytes = [], []
+        for name, lst in (("a", offs_t), ("b", two_t)):
+            picked = sb("xs_" + name, [P, S], U8)
+            nc.vector.tensor_copy(picked[:], xs_table[:].indirect(lst[:]))
+            x_bytes.append(picked)
+        for name, lst in (("a", offs_t), ("b", two_t)):
+            picked = sb("xw_" + name, [P, S], U32)
+            nc.vector.tensor_copy(picked[:], xw_table[:].bitcast(U32).indirect(lst[:]))
+            x_codes.append(picked)
+
+        front = {(m, h): sb("front%d%d" % (m, h), [P, P * PACK], BF16) for m in range(2) for h in range(2)}
+        back = [sb("back%d" % m, [P, 2, P * PACK], BF16) for m in range(2)]
+        w_codes, w_bytes = {}, {}
+
+        def cast_front(m, h, copy):
+            copy(
+                front[m, h][:].rearrange("p (t m j) -> p m j t", t=2, j=PACK),
+                raw[m, h][:].rearrange("p j (m t) -> p m j t", t=PACK)[:, :, :, 0:2],
+            )
+
+        def cast_back(m, h, copy):
+            copy(
+                back[m][:, :, h * HALF * PACK : (h + 1) * HALF * PACK].rearrange("p t (m j) -> p m j t", j=PACK),
+                raw[m, h][:].rearrange("p j (m t) -> p m j t", t=PACK)[:, :, :, 2:4],
+            )
+
+        def quantize_weight(m, name, src, blocks):
+            codes = sb("w_codes%d%s" % (m, name), [P, len(blocks) * P], U32)
+            scales = sb("w_bytes%d%s" % (m, name), [P, len(blocks) * P], U8)
+            nc.vector.quantize_mx(out=codes[:].bitcast(FP8X4), scales=scales[:], in_=src)
+            for i, block in enumerate(blocks):
+                w_codes[m, block] = codes[:, i * P : (i + 1) * P]
+                w_bytes[m, block] = scales[:, i * P : (i + 1) * P]
+
+        def quantize_front(m, h):
+            quantize_weight(m, "front%d" % h, front[m, h][:], (h,))
+
+        def quantize_back(m):
+            quantize_weight(m, "back", back[m][:].rearrange("p t c -> p (t c)"), (2, 3))
+
+        y = {}
+
+        def first_product(block):
+            acc = psum.tile([P, S], F32, name="y_acc", tag="y_acc", bufs=2)
+            for m in range(2):
+                nc.tensor.matmul_mx(
+                    out=acc[:],
+                    lhsT=w_codes[m, block].bitcast(FP8X4),
+                    lhsT_scale=w_bytes[m, block],
+                    rhs=x_codes[m][:].bitcast(FP8X4),
+                    rhs_scale=x_bytes[m][:],
+                    start=(m == 0),
+                    stop=(m == 1),
+                )
+            y[block] = sb("y%d" % block, [P, S], F32)
+            nc.vector.tensor_copy(y[block][:], acc[:])
+
+        pairs, sums, larger, ub = {}, {}, {}, {}
+
+        def fetch_pairs(block):
+            pairs[block] = sb("pairs%d" % block, [P, 2, W], F32)
+            nc.scalar.activation(pairs[block][:, 0, :], y[block][:].indirect(n1_t[:]), COPY)
+            nc.scalar.activation(pairs[block][:, 1, :], y[block][:].indirect(n2_t[:]), COPY)
+            left, right = pairs[block][:, 0, :], pairs[block][:, 1, :]
+            sums[block] = sb("sums%d" % block, [P, W], F32, tag=("w1_hi", "w_codes1back", "w_codes0back", "")[block])
+            nc.vector.tensor_tensor(sums[block][:], left, right, ALU.add)
+
+        def take_larger(block):
+            left, right = pairs[block][:, 0, :], pairs[block][:, 1, :]
+            larger[block] = sb("larger%d" % block, [P, W], F32, tag=("", "w_bytes1back", "w_bytes0back", "")[block])
+            nc.vector.tensor_tensor(larger[block][:], left, right, ALU.max)
+
+        def put_sum(block):
+            ub[block] = sb("ub%d" % block, [P, S], F32)
+            nc.scalar.activation(ub[block][:].indirect(n3_t[:]), sums[block][:], COPY)
+
+        def put_max(block):
+            nc.scalar.activation(ub[block][:].indirect(n4_t[:]), larger[block][:], COPY)
+
+        dealt = {t: sb("dealt%d" % t, [P, S], F32) for t in range(2)}
+        z_round = [sb("z_round%d" % h, [P, W * PACK], BF16) for h in range(2)]
+        kept = [sb("kept%d" % u, [P, 2, S], F32) for u in range(2)]
+        far = [sb("far%d" % u, [P, 2, S], F32) for u in range(2)]
+
+        def deal_rows(block):
+            for t in range(2):
+                nc.sync.dma_start(dealt[t][block * HALF : (block + 1) * HALF, :], ub[block][t * HALF : (t + 1) * HALF, :])
+
+        def weigh(t):
+            rows = dealt[t] if t < 2 else ub[t]
+            nc.vector.tensor_scalar(kept[t // 2][:, t % 2, :], rows[:], gs_t[:, t : t + 1], None, ALU.mult)
+
+        def fetch_far(t, h):
+            window = kept[t // 2][:, t % 2, :]
+            nc.scalar.activation(far[t // 2][:, t % 2, h * W : (h + 1) * W], window.indirect(n5_t[:, 8 * h : 8 * h + 8]), COPY)
+
+        def make_z(u, h):
+            cols = slice(h * W, (h + 1) * W)
+            nc.vector.tensor_tensor(
+                z_round[h][:].rearrange("p (c t) -> p c t", t=PACK)[:, :, 2 * u : 2 * u + 2],
+                kept[u][:, :, cols].rearrange("p t c -> p c t"),
+                far[u][:, :, cols].rearrange("p t c -> p c t"),
+                ALU.subtract,
+            )
+
+        d_codes = {}
+        d_bytes = sb("d_bytes", [P, 2, H], U8)
+
+        def pick_code_bytes():
+            d_picked = sb("ds_picked", [P, 2, H], U8, tag="pairs1")
+            for h in range(2):
+                for i, lst in enumerate((ka_t, kb_t)):
+                    nc.vector.tensor_copy(
+                        d_picked[:, i, h * (H // 2) : (h + 1) * (H // 2)],
+                        ds_table[:].indirect(lst[:, 16 * h : 16 * h + 16]),
+                    )
+            plane = d_bytes[:].rearrange("p i c -> p (i c)").bitcast(I32)
+            nc.vector.memset(plane, 0)
+            picked = d_picked[:].rearrange("p i c -> p (i c)").bitcast(I32)
+            for r in range(4):
+                src = 16 * (r // 2) + r % 2
+                nc.sync.dma_start(plane[r:P:32, :], picked[src:P:32, :])
+
+        def pick_code_words(h):
+            d_codes[h] = sb("d_codes%d" % h, [P, 2, H // 2], U32, tag=("pairs2", "other0")[h])
+            for i, lst in enumerate((ka_t, kb_t)):
+                nc.vector.tensor_copy(d_codes[h][:, i, :], dw_table[:].bitcast(U32).indirect(lst[:, 16 * h : 16 * h + 16]))
+
+        z_codes = sb("z_codes", [P, S], U32)
+        z_bytes = sb("z_bytes", [P, S], U8)
+
+        def quantize_z(h):
+            cols = slice(h * W, (h + 1) * W)
+            nc.vector.quantize_mx(out=z_codes[:, cols].bitcast(FP8X4), scales=z_bytes[:, cols], in_=z_round[h][:])
+
+        h2 = {}
+
+        def second_product(block, cols, name):
+            n = cols.stop - cols.start
+            acc = psum.tile([P, n], F32, name=name, tag=name)
+            rows = slice((block % 2) * P, (block % 2 + 1) * P)
+            for i in range(2):
+                nc.tensor.matmul_mx(
+                    out=acc[:],
+                    lhsT=d_codes[block // 2][:, i, rows].bitcast(FP8X4),
+                    lhsT_scale=d_bytes[:, i, block * P : (block + 1) * P],
+                    rhs=z_codes[:, cols].bitcast(FP8X4),
+                    rhs_scale=z_bytes[:, cols],
+                    start=(i == 0),
+                    stop=(i == 1),
+                )
+            if block not in h2:
+                h2[block] = sb("h2_%d" % block, [P, S], F32)
+            nc.vector.tensor_scalar(h2[block][:, cols], acc[:], 0.0625, None, ALU.mult)
+
+        other, ends, page = {}, {}, {}
+
+        def fetch_other(block):
+            other[block] = sb("other%d" % block, [P, S], F32)
+            for h in range(2):
+                nc.scalar.activation(other[block][:, h * W : (h + 1) * W], h2[block][:].indirect(n8_t[:, 8 * h : 8 * h + 8]), COPY)
+            ends[block] = sb("ends%d" % block, [P, 2, S], F32)
+            nc.vector.tensor_tensor(ends[block][:, 0, :], h2[block][:], other[block][:], ALU.max)
+            nc.vector.tensor_tensor(ends[block][:, 1, :], h2[block][:], other[block][:], ALU.min)
+
+        def put_larger(block):
+            page[block] = sb("page%d" % block, [P, U], F32)
+            nc.scalar.activation(page[block][:].indirect(n6_t[:]), ends[block][:, 0, :], COPY)
+
+        def put_smaller(block):
+            nc.scalar.activation(page[block][:].indirect(n7_t[:]), ends[block][:, 1, :], COPY)
+            nc.sync.dma_start(out[block * P : (block + 1) * P, :], page[block][:])
+
+        cast_front(0, 0, nc.scalar.copy)
+        quantize_front(0, 0)
+        cast_front(1, 0, nc.vector.tensor_copy)
+        quantize_front(1, 0)
+        first_product(0)
+        cast_back(0, 0, nc.scalar.copy)
+        cast_back(1, 0, nc.scalar.copy)
+        cast_front(0, 1, nc.vector.tensor_copy)
+        cast_back(0, 1, nc.vector.tensor_copy)
+        fetch_pairs(0)
+        take_larger(0)
+        cast_front(1, 1, nc.vector.tensor_copy)
+        for m in range(2):
+            quantize_front(m, 1)
+        first_product(1)
+        put_sum(0)
+        put_max(0)
+        deal_rows(0)
+        cast_back(1, 1, nc.vector.tensor_copy)
+        for m in range(2):
+            quantize_back(m)
+        for block in (2, 3):
+            first_product(block)
+        for block in (1, 2, 3):
+            fetch_pairs(block)
+            take_larger(block)
+        pick_code_bytes()
+        pick_code_words(0)
+        put_sum(1)
+        put_max(1)
+        deal_rows(1)
+        put_sum(2)
+        put_sum(3)
+        put_max(2)
+        put_max(3)
+        for t in (2, 3, 0, 1):
+            weigh(t)
+        for u in (1, 0):
+            for h in range(2):
+                for t in (2 * u, 2 * u + 1):
+                    fetch_far(t, h)
+                make_z(u, h)
+        for h in range(2):
+            quantize_z(h)
+            second_product(0, slice(h * W, (h + 1) * W), "h_first%d" % h)
+        second_product(1, slice(0, S), "h_acc1")
+        fetch_other(0)
+        fetch_other(1)
+        pick_code_words(1)
+        for block in (2, 3):
+            second_product(block, slice(0, S), "h_acc%d" % block)
+        put_larger(0)
+        put_larger(1)
+        put_smaller(0)
+        fetch_other(2)
+        put_smaller(1)
+        fetch_other(3)
+        put_larger(2)
+        put_larger(3)
+        put_smaller(2)
+        put_smaller(3)

@@ -50,7 +50,7 @@ def tile_picked_dttzacphdpagmx_none_p_kernel(
         nc.sync.dma_start(xw_table[:], x_words[0].rearrange("p n t -> p (n t)").bitcast(I32))
         xs_rows = x_scales[0].bitcast(I32)
         for r in range(4):
-            nc.scalar.dma_start(xs_table[r:P:32, :].bitcast(I32), xs_rows[r:16:4, :])
+            nc.sync.dma_start(xs_table[r:P:32, :].bitcast(I32), xs_rows[r:16:4, :])
         raw = {}
         raw[0, 0] = load_weight_half("w1_lo", w1, 0, nc.sync)
         raw[1, 0] = load_weight_half("w2_lo", w2, 0, nc.sync)
@@ -119,7 +119,7 @@ def tile_picked_dttzacphdpagmx_none_p_kernel(
         y = {}
 
         def first_product(block):
-            acc = psum.tile([P, S], F32, name="y_acc", tag="y_acc", bufs=2)
+            acc = psum.tile([P, S], F32, name="y_acc", tag="whole", bufs=4)
             for m in range(2):
                 nc.tensor.matmul_mx(
                     out=acc[:],
@@ -145,7 +145,7 @@ def tile_picked_dttzacphdpagmx_none_p_kernel(
 
         def take_larger(block):
             left, right = pairs[block][:, 0, :], pairs[block][:, 1, :]
-            larger[block] = sb("larger%d" % block, [P, W], F32, tag=("", "w_bytes1back", "w_bytes0back", "")[block])
+            larger[block] = sb("larger%d" % block, [P, W], F32, tag=("front01", "w_bytes1back", "w_bytes0back", "")[block])
             nc.vector.tensor_tensor(larger[block][:], left, right, ALU.max)
 
         def put_sum(block):
@@ -156,9 +156,7 @@ def tile_picked_dttzacphdpagmx_none_p_kernel(
             nc.scalar.activation(ub[block][:].indirect(n4_t[:]), larger[block][:], COPY)
 
         dealt = {t: sb("dealt%d" % t, [P, S], F32) for t in range(2)}
-        z_round = [sb("z_round%d" % h, [P, W * PACK], BF16) for h in range(2)]
         kept = [sb("kept%d" % u, [P, 2, S], F32) for u in range(2)]
-        far = [sb("far%d" % u, [P, 2, S], F32) for u in range(2)]
 
         def deal_rows(block):
             for t in range(2):
@@ -175,7 +173,7 @@ def tile_picked_dttzacphdpagmx_none_p_kernel(
         def make_z(u, h):
             cols = slice(h * W, (h + 1) * W)
             nc.vector.tensor_tensor(
-                z_round[h][:].rearrange("p (c t) -> p c t", t=PACK)[:, :, 2 * u : 2 * u + 2],
+                z_round[:, cols, 2 * u : 2 * u + 2],
                 kept[u][:, :, cols].rearrange("p t c -> p c t"),
                 far[u][:, :, cols].rearrange("p t c -> p c t"),
                 ALU.subtract,
@@ -192,6 +190,9 @@ def tile_picked_dttzacphdpagmx_none_p_kernel(
                         d_picked[:, i, h * (H // 2) : (h + 1) * (H // 2)],
                         ds_table[:].indirect(lst[:, 16 * h : 16 * h + 16]),
                     )
+            return d_picked
+
+        def place_code_bytes(d_picked):
             plane = d_bytes[:].rearrange("p i c -> p (i c)").bitcast(I32)
             nc.vector.memset(plane, 0)
             picked = d_picked[:].rearrange("p i c -> p (i c)").bitcast(I32)
@@ -209,13 +210,13 @@ def tile_picked_dttzacphdpagmx_none_p_kernel(
 
         def quantize_z(h):
             cols = slice(h * W, (h + 1) * W)
-            nc.vector.quantize_mx(out=z_codes[:, cols].bitcast(FP8X4), scales=z_bytes[:, cols], in_=z_round[h][:])
+            nc.vector.quantize_mx(out=z_codes[:, cols].bitcast(FP8X4), scales=z_bytes[:, cols], in_=z_round[:, cols, :].rearrange("p c t -> p (c t)"))
 
-        h2 = {}
+        h2 = [sb("h2_%d" % u, [P, 2, S], F32) for u in range(2)]
 
         def second_product(block, cols, name):
             n = cols.stop - cols.start
-            acc = psum.tile([P, n], F32, name=name, tag=name)
+            acc = psum.tile([P, n], F32, name=name, tag="whole" if n == S else "half", bufs=4)
             rows = slice((block % 2) * P, (block % 2 + 1) * P)
             for i in range(2):
                 nc.tensor.matmul_mx(
@@ -227,26 +228,28 @@ def tile_picked_dttzacphdpagmx_none_p_kernel(
                     start=(i == 0),
                     stop=(i == 1),
                 )
-            if block not in h2:
-                h2[block] = sb("h2_%d" % block, [P, S], F32)
-            nc.vector.tensor_scalar(h2[block][:, cols], acc[:], 0.0625, None, ALU.mult)
+            nc.vector.tensor_scalar(h2[block // 2][:, block % 2, cols], acc[:], 0.0625, None, ALU.mult)
 
-        other, ends, page = {}, {}, {}
+        other = [sb("other%d" % u, [P, 2, S], F32) for u in range(2)]
+        up, down, page = {}, {}, {}
 
         def fetch_other(block):
-            other[block] = sb("other%d" % block, [P, S], F32)
+            rows, fetched = h2[block // 2][:, block % 2, :], other[block // 2][:, block % 2, :]
             for h in range(2):
-                nc.scalar.activation(other[block][:, h * W : (h + 1) * W], h2[block][:].indirect(n8_t[:, 8 * h : 8 * h + 8]), COPY)
-            ends[block] = sb("ends%d" % block, [P, 2, S], F32)
-            nc.vector.tensor_tensor(ends[block][:, 0, :], h2[block][:], other[block][:], ALU.max)
-            nc.vector.tensor_tensor(ends[block][:, 1, :], h2[block][:], other[block][:], ALU.min)
+                nc.scalar.activation(fetched[:, h * W : (h + 1) * W], rows.indirect(n8_t[:, 8 * h : 8 * h + 8]), COPY)
+            up[block] = sb("up%d" % block, [P, S], F32)
+            nc.vector.tensor_tensor(up[block][:], rows, fetched, ALU.max)
+
+        def take_smaller(u):
+            down[u] = sb("down%d" % u, [P, 2, S], F32)
+            nc.vector.tensor_tensor(down[u][:], h2[u][:], other[u][:], ALU.min)
 
         def put_larger(block):
             page[block] = sb("page%d" % block, [P, U], F32)
-            nc.scalar.activation(page[block][:].indirect(n6_t[:]), ends[block][:, 0, :], COPY)
+            nc.scalar.activation(page[block][:].indirect(n6_t[:]), up[block][:], COPY)
 
         def put_smaller(block):
-            nc.scalar.activation(page[block][:].indirect(n7_t[:]), ends[block][:, 1, :], COPY)
+            nc.scalar.activation(page[block][:].indirect(n7_t[:]), down[block // 2][:, block % 2, :], COPY)
             nc.sync.dma_start(out[block * P : (block + 1) * P, :], page[block][:])
 
         cast_front(0, 0, nc.scalar.copy)
@@ -258,16 +261,16 @@ def tile_picked_dttzacphdpagmx_none_p_kernel(
         cast_back(1, 0, nc.scalar.copy)
         cast_front(0, 1, nc.vector.tensor_copy)
         cast_back(0, 1, nc.vector.tensor_copy)
+        quantize_front(0, 1)
         fetch_pairs(0)
         take_larger(0)
         cast_front(1, 1, nc.vector.tensor_copy)
-        for m in range(2):
-            quantize_front(m, 1)
+        quantize_front(1, 1)
         first_product(1)
         put_sum(0)
+        cast_back(1, 1, nc.vector.tensor_copy)
         put_max(0)
         deal_rows(0)
-        cast_back(1, 1, nc.vector.tensor_copy)
         for m in range(2):
             quantize_back(m)
         for block in (2, 3):
@@ -275,17 +278,20 @@ def tile_picked_dttzacphdpagmx_none_p_kernel(
         for block in (1, 2, 3):
             fetch_pairs(block)
             take_larger(block)
-        pick_code_bytes()
+        d_picked = pick_code_bytes()
         pick_code_words(0)
         put_sum(1)
         put_max(1)
         deal_rows(1)
+        place_code_bytes(d_picked)
         put_sum(2)
         put_sum(3)
         put_max(2)
         put_max(3)
         for t in (2, 3, 0, 1):
             weigh(t)
+        z_round = sb("z_round", [P, S, PACK], BF16, tag="ub1")
+        far = [sb("far%d" % u, [P, 2, S], F32, tag=("dealt1", "")[u]) for u in range(2)]
         for u in (1, 0):
             for h in range(2):
                 for t in (2 * u, 2 * u + 1):
@@ -293,20 +299,18 @@ def tile_picked_dttzacphdpagmx_none_p_kernel(
                 make_z(u, h)
         for h in range(2):
             quantize_z(h)
-            second_product(0, slice(h * W, (h + 1) * W), "h_first%d" % h)
-        second_product(1, slice(0, S), "h_acc1")
-        fetch_other(0)
-        fetch_other(1)
-        pick_code_words(1)
-        for block in (2, 3):
-            second_product(block, slice(0, S), "h_acc%d" % block)
-        put_larger(0)
-        put_larger(1)
-        put_smaller(0)
-        fetch_other(2)
-        put_smaller(1)
-        fetch_other(3)
-        put_larger(2)
-        put_larger(3)
-        put_smaller(2)
-        put_smaller(3)
+            for block in range(2):
+                second_product(block, slice(h * W, (h + 1) * W), "h_half%d%d" % (block, h))
+        for u in range(2):
+            blocks = (2 * u, 2 * u + 1)
+            if u == 1:
+                pick_code_words(1)
+                for block in blocks:
+                    second_product(block, slice(0, S), "h_whole%d" % block)
+            for block in blocks:
+                fetch_other(block)
+            take_smaller(u)
+            for block in blocks:
+                put_larger(block)
+            for block in blocks:
+                put_smaller(block)

@@ -43,14 +43,14 @@ def tile_picked_dttzacphdpagmx_none_p_kernel(
             return raw
 
         xs_table = sb("xs_table", [P, T], U8)
-        nc.gpsimd.memset(xs_table[:].bitcast(I32), 0)
+        nc.vector.memset(xs_table[:].bitcast(I32), 0)
         offs_t = load_list("offs_t", offs)
         two_t = load_list("two_t", two)
-        xw_table = sb("xw_table", [P, T], I32)
-        nc.sync.dma_start(xw_table[:], x_words[0].rearrange("p n t -> p (n t)").bitcast(I32))
         xs_rows = x_scales[0].bitcast(I32)
         for r in range(4):
             nc.sync.dma_start(xs_table[r:P:32, :].bitcast(I32), xs_rows[r:16:4, :])
+        xw_table = sb("xw_table", [P, T], I32)
+        nc.sync.dma_start(xw_table[:], x_words[0].rearrange("p n t -> p (n t)").bitcast(I32))
         raw = {}
         raw[0, 0] = load_weight_half("w1_lo", w1, 0, nc.sync)
         raw[1, 0] = load_weight_half("w2_lo", w2, 0, nc.sync)
@@ -156,7 +156,7 @@ def tile_picked_dttzacphdpagmx_none_p_kernel(
             nc.scalar.activation(ub[block][:].indirect(n4_t[:]), larger[block][:], COPY)
 
         dealt = {t: sb("dealt%d" % t, [P, S], F32) for t in range(2)}
-        kept = [sb("kept%d" % u, [P, 2, S], F32) for u in range(2)]
+        kept = {}
 
         def deal_rows(block):
             for t in range(2):
@@ -166,16 +166,14 @@ def tile_picked_dttzacphdpagmx_none_p_kernel(
             rows = dealt[t] if t < 2 else ub[t]
             nc.vector.tensor_scalar(kept[t // 2][:, t % 2, :], rows[:], gs_t[:, t : t + 1], None, ALU.mult)
 
-        def fetch_far(t, h):
-            window = kept[t // 2][:, t % 2, :]
-            nc.scalar.activation(far[t // 2][:, t % 2, h * W : (h + 1) * W], window.indirect(n5_t[:, 8 * h : 8 * h + 8]), COPY)
-
-        def make_z(u, h):
-            cols = slice(h * W, (h + 1) * W)
+        def make_z(u, cols, far):
+            entries = n5_t[:, cols.start // 16 : cols.stop // 16]
+            for e in range(2):
+                nc.scalar.activation(far[:, e, :], kept[u][:, e, :].indirect(entries), COPY)
             nc.vector.tensor_tensor(
                 z_round[:, cols, 2 * u : 2 * u + 2],
                 kept[u][:, :, cols].rearrange("p t c -> p c t"),
-                far[u][:, :, cols].rearrange("p t c -> p c t"),
+                far.rearrange("p t c -> p c t"),
                 ALU.subtract,
             )
 
@@ -208,8 +206,7 @@ def tile_picked_dttzacphdpagmx_none_p_kernel(
         z_codes = sb("z_codes", [P, S], U32)
         z_bytes = sb("z_bytes", [P, S], U8)
 
-        def quantize_z(h):
-            cols = slice(h * W, (h + 1) * W)
+        def quantize_z(cols):
             nc.vector.quantize_mx(out=z_codes[:, cols].bitcast(FP8X4), scales=z_bytes[:, cols], in_=z_round[:, cols, :].rearrange("p c t -> p (c t)"))
 
         h2 = [sb("h2_%d" % u, [P, 2, S], F32) for u in range(2)]
@@ -288,19 +285,19 @@ def tile_picked_dttzacphdpagmx_none_p_kernel(
         put_sum(3)
         put_max(2)
         put_max(3)
-        for t in (2, 3, 0, 1):
-            weigh(t)
-        z_round = sb("z_round", [P, S, PACK], BF16, tag="ub1")
-        far = [sb("far%d" % u, [P, 2, S], F32, tag=("dealt1", "")[u]) for u in range(2)]
-        for u in (1, 0):
-            for h in range(2):
-                for t in (2 * u, 2 * u + 1):
-                    fetch_far(t, h)
-                make_z(u, h)
+        for u in range(2):
+            kept[u] = sb("kept%d" % u, [P, 2, S], F32, tag=("", "dealt1")[u])
+            for t in (2 * u, 2 * u + 1):
+                weigh(t)
+        z_round = sb("z_round", [P, S, PACK], BF16)
         for h in range(2):
-            quantize_z(h)
+            cols = slice(h * W, (h + 1) * W)
+            far = sb("far%d" % h, [P, 2, 2, W], F32, tag=("", "ub3")[h])
+            for u in range(2):
+                make_z(u, cols, far[:, u])
+            quantize_z(cols)
             for block in range(2):
-                second_product(block, slice(h * W, (h + 1) * W), "h_half%d%d" % (block, h))
+                second_product(block, cols, "h_half%d%d" % (block, h))
         for u in range(2):
             blocks = (2 * u, 2 * u + 1)
             if u == 1:

@@ -43,15 +43,15 @@ def tile_picked_dttzacphdpagmx_none_p_kernel(
             return raw
 
         xs_table = sb("xs_table", [P, T], U8)
-        nc.vector.memset(xs_table[:].bitcast(I32), 0)
+        nc.gpsimd.memset(xs_table[:].bitcast(I32), 0)
+        raw = {}
         offs_t = load_list("offs_t", offs)
-        two_t = load_list("two_t", two)
-        xs_rows = x_scales[0].bitcast(I32)
-        for r in range(4):
-            nc.sync.dma_start(xs_table[r:P:32, :].bitcast(I32), xs_rows[r:16:4, :])
         xw_table = sb("xw_table", [P, T], I32)
         nc.sync.dma_start(xw_table[:], x_words[0].rearrange("p n t -> p (n t)").bitcast(I32))
-        raw = {}
+        xs_rows = x_scales[0].bitcast(I32)
+        for r in range(4):
+            nc.scalar.dma_start(xs_table[r:P:32, :].bitcast(I32), xs_rows[r:16:4, :])
+        two_t = load_list("two_t", two)
         raw[0, 0] = load_weight_half("w1_lo", w1, 0, nc.sync)
         raw[1, 0] = load_weight_half("w2_lo", w2, 0, nc.sync)
         n1_t = load_list("n1_t", n1)

@@ -209,7 +209,8 @@ def tile_picked_dttzacphdpagmx_none_p_kernel(
         def quantize_z(cols):
             nc.vector.quantize_mx(out=z_codes[:, cols].bitcast(FP8X4), scales=z_bytes[:, cols], in_=z_round[:, cols, :].rearrange("p c t -> p (c t)"))
 
-        h2 = [sb("h2_%d" % u, [P, 2, S], F32) for u in range(2)]
+        h2 = sb("h2", [P, 4, S], F32)
+        place = (3, 2, 0, 1)
 
         def second_product(block, cols, name):
             n = cols.stop - cols.start
@@ -225,29 +226,35 @@ def tile_picked_dttzacphdpagmx_none_p_kernel(
                     start=(i == 0),
                     stop=(i == 1),
                 )
-            nc.vector.tensor_scalar(h2[block // 2][:, block % 2, cols], acc[:], 0.0625, None, ALU.mult)
+            nc.vector.tensor_scalar(h2[:, place[block], cols], acc[:], 0.0625, None, ALU.mult)
 
         other = [sb("other%d" % u, [P, 2, S], F32) for u in range(2)]
         up, down, page = {}, {}, {}
 
         def fetch_other(block):
-            rows, fetched = h2[block // 2][:, block % 2, :], other[block // 2][:, block % 2, :]
-            for h in range(2):
-                nc.scalar.activation(fetched[:, h * W : (h + 1) * W], rows.indirect(n8_t[:, 8 * h : 8 * h + 8]), COPY)
+            at = place[block]
+            rows, fetched = h2[:, at, :], other[block // 2][:, at % 2, :]
+            if at < 3:
+                window = h2[:, at : at + 2, :].rearrange("p b c -> p (b c)")
+                nc.scalar.activation(fetched, window.indirect(n8_t[:]), COPY)
+            else:
+                for h in range(2):
+                    nc.scalar.activation(fetched[:, h * W : (h + 1) * W], rows.indirect(n8_t[:, 8 * h : 8 * h + 8]), COPY)
             up[block] = sb("up%d" % block, [P, S], F32)
             nc.vector.tensor_tensor(up[block][:], rows, fetched, ALU.max)
 
         def take_smaller(u):
             down[u] = sb("down%d" % u, [P, 2, S], F32)
-            nc.vector.tensor_tensor(down[u][:], h2[u][:], other[u][:], ALU.min)
+            nc.vector.tensor_tensor(down[u][:], h2[:, 2 - 2 * u : 4 - 2 * u, :], other[u][:], ALU.min)
 
         def put_larger(block):
             page[block] = sb("page%d" % block, [P, U], F32)
             nc.scalar.activation(page[block][:].indirect(n6_t[:]), up[block][:], COPY)
 
         def put_smaller(block):
-            nc.scalar.activation(page[block][:].indirect(n7_t[:]), down[block // 2][:, block % 2, :], COPY)
-            nc.sync.dma_start(out[block * P : (block + 1) * P, :], page[block][:])
+            nc.scalar.activation(page[block][:].indirect(n7_t[:]), down[block // 2][:, place[block] % 2, :], COPY)
+            queue = nc.scalar if block == 3 else nc.sync
+            queue.dma_start(out[block * P : (block + 1) * P, :], page[block][:])
 
         cast_front(0, 0, nc.scalar.copy)
         quantize_front(0, 0)

from contextlib import ExitStack

import concourse.mybir as mybir

K, T, S, H, W, G, U = 512, 1024, 256, 512, 128, 2048, 512
FLOPS = 2 * (2 * K * H * S) + 2 * (2 * K * H * S)

F32 = mybir.dt.float32
BF16 = mybir.dt.bfloat16
I32 = mybir.dt.int32
U32 = mybir.dt.uint32
U16 = mybir.dt.uint16
U8 = mybir.dt.uint8
FP8X4 = mybir.dt.float8_e4m3fn_x4
ALU = mybir.AluOpType
COPY = mybir.ActivationFunctionType.Copy

P = 128
PACK = 4
HALF = 64


def tile_picked_dttzacphdpagmx_none_p_kernel(
    tc, x_words, x_scales, w1, w2, gs, d_words, d_scales, offs, two, n1, n2, n3, n4, n5, ka, kb, n6, n7, n8, out
):
    nc = tc.nc
    with ExitStack() as ctx:
        keep = ctx.enter_context(tc.tile_pool(name="keep", bufs=1))
        psum = ctx.enter_context(tc.psum_pool(name="psum", bufs=1))

        def sb(name, shape, dtype, tag=""):
            return keep.tile(shape, dtype, name=name, tag=tag or name, align_bytes=64)

        def load_list(name, src):
            tile = keep.tile(list(src.shape), U16, name=name)
            nc.sync.dma_start(tile[:], src)
            return tile

        def load_weight_half(name, w, half, queue):
            raw = sb(name, [P, PACK, H // 2], F32)
            cols = slice(half * (H // 2), (half + 1) * (H // 2))
            queue.dma_start(raw[:], w.rearrange("(p j) c -> p j c", j=PACK)[:, :, cols])
            return raw

        xs_table = sb("xs_table", [P, T], U8)
        nc.gpsimd.memset(xs_table[:].bitcast(I32), 0)
        raw = {}
        offs_t = load_list("offs_t", offs)
        xw_table = sb("xw_table", [P, T], I32)
        nc.sync.dma_start(xw_table[:], x_words[0].rearrange("p n t -> p (n t)").bitcast(I32))
        xs_rows = x_scales[0].bitcast(I32)
        for r in range(4):
            nc.scalar.dma_start(xs_table[r:P:32, :].bitcast(I32), xs_rows[r:16:4, :])
        two_t = load_list("two_t", two)
        raw[0, 0] = load_weight_half("w1_lo", w1, 0, nc.sync)
        raw[1, 0] = load_weight_half("w2_lo", w2, 0, nc.sync)
        n1_t = load_list("n1_t", n1)
        n2_t = load_list("n2_t", n2)
        raw[0, 1] = load_weight_half("w1_hi", w1, 1, nc.sync)
        raw[1, 1] = load_weight_half("w2_hi", w2, 1, nc.sync)
        n3_t = load_list("n3_t", n3)
        n4_t = load_list("n4_t", n4)
        ka_t = load_list("ka_t", ka)
        kb_t = load_list("kb_t", kb)
        ds_table = sb("ds_table", [P, G], U8)
        nc.vector.memset(ds_table[:].bitcast(I32), 0)
        ds_rows = d_scales[0].bitcast(I32)
        for e in range(2):
            nc.sync.dma_start(ds_table[e:P:16, :].bitcast(I32), ds_rows[e:16:2, :])
        dw_table = sb("dw_table", [P, G], I32)
        nc.sync.dma_start(dw_table[:], d_words[0].rearrange("p n t -> p (n t)").bitcast(I32))
        gs_t = sb("gs_t", [P, PACK], F32)
        nc.sync.dma_start(gs_t[:], gs.rearrange("(p t) o -> p (t o)", t=PACK))
        n5_t = load_list("n5_t", n5)
        n8_t = load_list("n8_t", n8)
        n6_t = load_list("n6_t", n6)
        n7_t = load_list("n7_t", n7)

        x_codes, x_bytes = [], []
        for name, lst in (("a", offs_t), ("b", two_t)):
            picked = sb("xs_" + name, [P, S], U8)
            nc.vector.tensor_copy(picked[:], xs_table[:].indirect(lst[:]))
            x_bytes.append(picked)
        for name, lst in (("a", offs_t), ("b", two_t)):
            picked = sb("xw_" + name, [P, S], U32)
            nc.vector.tensor_copy(picked[:], xw_table[:].bitcast(U32).indirect(lst[:]))
            x_codes.append(picked)

        front = {(m, h): sb("front%d%d" % (m, h), [P, P * PACK], BF16) for m in range(2) for h in range(2)}
        back = [sb("back%d" % m, [P, 2, P * PACK], BF16) for m in range(2)]
        w_codes, w_bytes = {}, {}

        def cast_front(m, h, copy):
            copy(
                front[m, h][:].rearrange("p (t m j) -> p m j t", t=2, j=PACK),
                raw[m, h][:].rearrange("p j (m t) -> p m j t", t=PACK)[:, :, :, 0:2],
            )

        def cast_back(m, h, copy):
            copy(
                back[m][:, :, h * HALF * PACK : (h + 1) * HALF * PACK].rearrange("p t (m j) -> p m j t", j=PACK),
                raw[m, h][:].rearrange("p j (m t) -> p m j t", t=PACK)[:, :, :, 2:4],
            )

        def quantize_weight(m, name, src, blocks):
            codes = sb("w_codes%d%s" % (m, name), [P, len(blocks) * P], U32)
            scales = sb("w_bytes%d%s" % (m, name), [P, len(blocks) * P], U8)
            nc.vector.quantize_mx(out=codes[:].bitcast(FP8X4), scales=scales[:], in_=src)
            for i, block in enumerate(blocks):
                w_codes[m, block] = codes[:, i * P : (i + 1) * P]
                w_bytes[m, block] = scales[:, i * P : (i + 1) * P]

        def quantize_front(m, h):
            quantize_weight(m, "front%d" % h, front[m, h][:], (h,))

        def quantize_back(m):
            quantize_weight(m, "back", back[m][:].rearrange("p t c -> p (t c)"), (2, 3))

        y = {}

        def first_product(block):
            acc = psum.tile([P, S], F32, name="y_acc", tag="whole", bufs=4)
            for m in range(2):
                nc.tensor.matmul_mx(
                    out=acc[:],
                    lhsT=w_codes[m, block].bitcast(FP8X4),
                    lhsT_scale=w_bytes[m, block],
                    rhs=x_codes[m][:].bitcast(FP8X4),
                    rhs_scale=x_bytes[m][:],
                    start=(m == 0),
                    stop=(m == 1),
                )
            y[block] = sb("y%d" % block, [P, S], F32)
            nc.vector.tensor_copy(y[block][:], acc[:])

        pairs, sums, larger, ub = {}, {}, {}, {}

        def fetch_pairs(block):
            pairs[block] = sb("pairs%d" % block, [P, 2, W], F32)
            nc.scalar.activation(pairs[block][:, 0, :], y[block][:].indirect(n1_t[:]), COPY)
            nc.scalar.activation(pairs[block][:, 1, :], y[block][:].indirect(n2_t[:]), COPY)
            left, right = pairs[block][:, 0, :], pairs[block][:, 1, :]
            sums[block] = sb("sums%d" % block, [P, W], F32, tag=("w1_hi", "w_codes1back", "w_codes0back", "")[block])
            nc.vector.tensor_tensor(sums[block][:], left, right, ALU.add)

        def take_larger(block):
            left, right = pairs[block][:, 0, :], pairs[block][:, 1, :]
            larger[block] = sb("larger%d" % block, [P, W], F32, tag=("front01", "w_bytes1back", "w_bytes0back", "")[block])
            nc.vector.tensor_tensor(larger[block][:], left, right, ALU.max)

        def put_sum(block):
            ub[block] = sb("ub%d" % block, [P, S], F32)
            nc.scalar.activation(ub[block][:].indirect(n3_t[:]), sums[block][:], COPY)

        def put_max(block):
            nc.scalar.activation(ub[block][:].indirect(n4_t[:]), larger[block][:], COPY)

        dealt = {t: sb("dealt%d" % t, [P, S], F32) for t in range(2)}
        kept = {}

        def deal_rows(block):
            for t in range(2):
                nc.sync.dma_start(dealt[t][block * HALF : (block + 1) * HALF, :], ub[block][t * HALF : (t + 1) * HALF, :])

        def weigh(t):
            rows = dealt[t] if t < 2 else ub[t]
            nc.vector.tensor_scalar(kept[t // 2][:, t % 2, :], rows[:], gs_t[:, t : t + 1], None, ALU.mult)

        def make_z(u, cols, far):
            entries = n5_t[:, cols.start // 16 : cols.stop // 16]
            for e in range(2):
                nc.scalar.activation(far[:, e, :], kept[u][:, e, :].indirect(entries), COPY)
            nc.vector.tensor_tensor(
                z_round[:, cols, 2 * u : 2 * u + 2],
                kept[u][:, :, cols].rearrange("p t c -> p c t"),
                far.rearrange("p t c -> p c t"),
                ALU.subtract,
            )

        d_codes = {}
        d_bytes = sb("d_bytes", [P, 2, H], U8)

        def pick_code_bytes():
            d_picked = sb("ds_picked", [P, 2, H], U8, tag="pairs1")
            for h in range(2):
                for i, lst in enumerate((ka_t, kb_t)):
                    nc.vector.tensor_copy(
                        d_picked[:, i, h * (H // 2) : (h + 1) * (H // 2)],
                        ds_table[:].indirect(lst[:, 16 * h : 16 * h + 16]),
                    )
            return d_picked

        def place_code_bytes(d_picked):
            plane = d_bytes[:].rearrange("p i c -> p (i c)").bitcast(I32)
            nc.vector.memset(plane, 0)
            picked = d_picked[:].rearrange("p i c -> p (i c)").bitcast(I32)
            for r in range(4):
                src = 16 * (r // 2) + r % 2
                nc.sync.dma_start(plane[r:P:32, :], picked[src:P:32, :])

        def pick_code_words(h):
            d_codes[h] = sb("d_codes%d" % h, [P, 2, H // 2], U32, tag=("pairs2", "other0")[h])
            for i, lst in enumerate((ka_t, kb_t)):
                nc.vector.tensor_copy(d_codes[h][:, i, :], dw_table[:].bitcast(U32).indirect(lst[:, 16 * h : 16 * h + 16]))

        z_codes = sb("z_codes", [P, S], U32)
        z_bytes = sb("z_bytes", [P, S], U8)

        def quantize_z(cols):
            nc.vector.quantize_mx(out=z_codes[:, cols].bitcast(FP8X4), scales=z_bytes[:, cols], in_=z_round[:, cols, :].rearrange("p c t -> p (c t)"))

        h2 = sb("h2", [P, 4, S], F32)
        place = (3, 2, 0, 1)

        def second_product(block, cols, name):
            n = cols.stop - cols.start
            acc = psum.tile([P, n], F32, name=name, tag="whole" if n == S else "half", bufs=4)
            rows = slice((block % 2) * P, (block % 2 + 1) * P)
            for i in range(2):
                nc.tensor.matmul_mx(
                    out=acc[:],
                    lhsT=d_codes[block // 2][:, i, rows].bitcast(FP8X4),
                    lhsT_scale=d_bytes[:, i, block * P : (block + 1) * P],
                    rhs=z_codes[:, cols].bitcast(FP8X4),
                    rhs_scale=z_bytes[:, cols],
                    start=(i == 0),
                    stop=(i == 1),
                )
            nc.vector.tensor_scalar(h2[:, place[block], cols], acc[:], 0.0625, None, ALU.mult)

        other = [sb("other%d" % u, [P, 2, S], F32) for u in range(2)]
        up, down, page = {}, {}, {}

        def fetch_other(block):
            at = place[block]
            rows, fetched = h2[:, at, :], other[block // 2][:, at % 2, :]
            if at < 3:
                window = h2[:, at : at + 2, :].rearrange("p b c -> p (b c)")
                nc.scalar.activation(fetched, window.indirect(n8_t[:]), COPY)
            else:
                for h in range(2):
                    nc.scalar.activation(fetched[:, h * W : (h + 1) * W], rows.indirect(n8_t[:, 8 * h : 8 * h + 8]), COPY)
            up[block] = sb("up%d" % block, [P, S], F32)
            nc.vector.tensor_tensor(up[block][:], rows, fetched, ALU.max)

        def take_smaller(u):
            down[u] = sb("down%d" % u, [P, 2, S], F32)
            nc.vector.tensor_tensor(down[u][:], h2[:, 2 - 2 * u : 4 - 2 * u, :], other[u][:], ALU.min)

        def put_larger(block):
            page[block] = sb("page%d" % block, [P, U], F32)
            nc.scalar.activation(page[block][:].indirect(n6_t[:]), up[block][:], COPY)

        def put_smaller(block):
            nc.scalar.activation(page[block][:].indirect(n7_t[:]), down[block // 2][:, place[block] % 2, :], COPY)
            queue = nc.scalar if block == 3 else nc.sync
            queue.dma_start(out[block * P : (block + 1) * P, :], page[block][:])

        cast_front(0, 0, nc.scalar.copy)
        quantize_front(0, 0)
        cast_front(1, 0, nc.vector.tensor_copy)
        quantize_front(1, 0)
        first_product(0)
        cast_back(0, 0, nc.scalar.copy)
        cast_back(1, 0, nc.scalar.copy)
        cast_front(0, 1, nc.vector.tensor_copy)
        cast_back(0, 1, nc.vector.tensor_copy)
        quantize_front(0, 1)
        fetch_pairs(0)
        take_larger(0)
        cast_front(1, 1, nc.vector.tensor_copy)
        quantize_front(1, 1)
        first_product(1)
        put_sum(0)
        cast_back(1, 1, nc.vector.tensor_copy)
        put_max(0)
        deal_rows(0)
        for m in range(2):
            quantize_back(m)
        for block in (2, 3):
            first_product(block)
        for block in (1, 2, 3):
            fetch_pairs(block)
            take_larger(block)
        d_picked = pick_code_bytes()
        pick_code_words(0)
        put_sum(1)
        put_max(1)
        deal_rows(1)
        place_code_bytes(d_picked)
        put_sum(2)
        put_sum(3)
        put_max(2)
        put_max(3)
        for u in range(2):
            kept[u] = sb("kept%d" % u, [P, 2, S], F32, tag=("", "dealt1")[u])
            for t in (2 * u, 2 * u + 1):
                weigh(t)
        z_round = sb("z_round", [P, S, PACK], BF16)
        for h in range(2):
            cols = slice(h * W, (h + 1) * W)
            far = sb("far%d" % h, [P, 2, 2, W], F32, tag=("", "ub3")[h])
            for u in range(2):
                make_z(u, cols, far[:, u])
            quantize_z(cols)
            for block in range(2):
                second_product(block, cols, "h_half%d%d" % (block, h))
        for u in range(2):
            blocks = (2 * u, 2 * u + 1)
            if u == 1:
                pick_code_words(1)
                for block in blocks:
                    second_product(block, slice(0, S), "h_whole%d" % block)
            for block in blocks:
                fetch_other(block)
            take_smaller(u)
            for block in blocks:
                put_larger(block)
            for block in blocks:
                put_smaller(block)
